import numpy as np, ml_dtypes
CORES = [7,15,23,31,135,143,151,159,167,175,183,191,199,207,215,223,231,239,247,255]
N = 20
T = 8
ROUTE = [[[3],[11],[19],[3],[18],[5],[5],[3]],[[3],[7],[3],[3],[8],[18],[3],[18]],[[3],[9],[3],[15],[2],[3],[8],[3]],[[3],[1],[10],[3],[3],[1],[3],[3]],[[3],[11],[3],[3],[5],[9],[4],[12]],[[3],[3],[3],[3],[13],[3],[4],[3]],[[11],[14],[3],[3],[3],[3],[3],[16]],[[3],[3],[3],[11],[4],[3],[5],[0]],[[3],[0],[14],[2],[19],[13],[18],[12]],[[6],[5],[3],[3],[5],[16],[3],[3]],[[6],[7],[7],[3],[3],[4],[3],[1]],[[5],[11],[3],[14],[7],[5],[1],[14]],[[19],[1],[14],[19],[3],[3],[3],[3]],[[8],[3],[3],[3],[14],[3],[3],[3]],[[3],[5],[4],[4],[3],[4],[3],[3]],[[12],[12],[15],[5],[3],[3],[11],[8]],[[3],[3],[3],[3],[4],[11],[3],[3]],[[3],[3],[9],[3],[14],[3],[7],[3]],[[3],[3],[16],[15],[3],[3],[6],[3]],[[8],[1],[14],[3],[3],[3],[3],[9]]]
CAP = 5
YW = 5
def setup_inputs(rng):
    return {"x": rng.standard_normal((N, 128, T), dtype=np.float32).astype(ml_dtypes.bfloat16)}
def reference(x):
    y = np.full((N, 128, YW), np.nan, x.dtype)
    fill = [0] * N
    for r in range(N):
        for t in range(T):
            for e in ROUTE[r][t]:
                if fill[e] < CAP:
                    y[e][:, fill[e]] = x[r][:, t]
                fill[e] += 1
    return {"y": y}

from concourse.bass import DstId, RemoteDMATransfer

SCRATCH = {
    "xs": ("sbuf", [128, 8], "bfloat16"),
    "land": ("sbuf", [128, 5], "bfloat16"),
}
SEMAPHORES = ["loaded", "sent", "arrived", "stored"]

OFF_CHIP_ENGINES = 8


def plan(tables, n):
    route, cap = tables["ROUTE"], tables["CAP"]
    fill = [0] * n
    runs = [[] for _ in range(n)]
    for r in range(n):
        for t in range(len(route[r])):
            for e in route[r][t]:
                if fill[e] < cap:
                    last = runs[r][-1] if runs[r] else None
                    if last and last[2] == e and last[0] + last[1] == t and last[3] + last[1] == fill[e]:
                        runs[r][-1] = (last[0], last[1] + 1, e, last[3])
                    else:
                        runs[r].append((t, 1, e, fill[e]))
                fill[e] += 1
    return [min(f, cap) for f in fill], runs


def calls_of(runs_r, r):
    calls = []
    for w in sorted(set(run[1] for run in runs_r if run[2] != r)):
        same = [run for run in runs_r if run[2] != r and run[1] == w]
        for i in range(0, len(same), OFF_CHIP_ENGINES):
            part = same[i:i + OFF_CHIP_ENGINES]
            eng = OFF_CHIP_ENGINES
            while eng * len(part) > OFF_CHIP_ENGINES:
                eng //= 2
            calls.append([(run, k * eng, eng) for k, run in enumerate(part)])
    return calls


def rank_program(g, core, T, topo):
    rank = T.rank_of(core)
    if rank is None:
        return
    n = len(T.cores)
    count, runs = plan(T.tables, n)
    calls = calls_of(runs[rank], rank)
    own = [run for run in runs[rank] if run[2] == rank]
    pad = count[rank] == 1
    width = 2 if pad else count[rank]

    if calls or own or pad:
        g.sync.dma_start(T.xs[:], T.x[:]).then_inc(T.sem.loaded, 16)
        g.sync.wait_ge(T.sem.loaded, 16)

    sent = 0
    if calls:
        g.wait_ge(T.sem.loaded, 16)
    for call in calls:
        transfers = []
        for (t0, w, e, s0), first, eng in call:
            rid, pid = topo.addr(T.cores[e], core)
            transfers.append(RemoteDMATransfer(
                dst_ids=[DstId(rid=rid, pnc=pid)], dma_engine_mask=((1 << eng) - 1) << first,
                remote_sem=T.sem.arrived, src=T.xs[:, t0:t0 + w], dst=T.land[:, s0:s0 + w]))
            sent += eng
        g.remote_dma_fused(transfers, local_sem=T.sem.sent)

    expect = 0
    for t0, w, e, s0 in own:
        g.sync.dma_start(T.land[:, s0:s0 + w], T.xs[:, t0:t0 + w]).then_inc(T.sem.arrived, 16)
        expect += 16
    if pad:
        g.sync.dma_start(T.land[:, 1:2], T.xs[:, 0:1]).then_inc(T.sem.arrived, 16)
        expect += 16

    for r in range(n):
        for call in calls_of(runs[r], r):
            expect += sum(eng for run, first, eng in call if run[2] == rank)
    if expect:
        g.sync.wait_ge(T.sem.arrived, expect)
    if width:
        g.sync.dma_start(T.y[:, 0:width], T.land[:, 0:width]).then_inc(T.sem.stored, 16)
        g.sync.wait_ge(T.sem.stored, 16)
    if sent:
        g.wait_ge(T.sem.sent, sent)
